import numpy as np
import ml_dtypes


def mxq(x, axis, fmt="e4m3"):
    dtype, down = {"e4m3": (ml_dtypes.float8_e4m3fn, 7), "e5m2": (ml_dtypes.float8_e5m2, 14)}[fmt]
    v = np.moveaxis(np.asarray(x, np.float32).astype(ml_dtypes.bfloat16).astype(np.float64), axis, -1)
    blocks = v.reshape(v.shape[:-1] + (-1, 32))
    amax = np.abs(blocks).max(-1, keepdims=True)
    byte = np.maximum(np.where(amax > 0, np.frexp(amax)[1] - 1 + 127, 0) - down, 1)
    scale = np.exp2(byte - 127.0)
    codes = (blocks / scale).astype(np.float32).astype(dtype).astype(np.float64)
    return np.moveaxis((codes * scale).reshape(v.shape), -1, axis)


WIDE = False


def mx_kscale(k):
    if not WIDE:
        return np.ones(k)
    levels = np.array([10, -10, 5, -5, 0])
    if k % 512:
        return np.exp2(np.random.permutation(np.resize(levels, k // 32))).repeat(32)
    a = np.empty((k // 512, 16))
    for p in range(k // 512):
        a[p, :8] = np.random.permutation(np.resize(levels, 8))
        for g in range(8):
            far = levels[np.abs(levels - a[p, g]) >= 10]
            a[p, g + 8] = far[np.random.randint(len(far))]
    return np.exp2(a.ravel()).repeat(32)


def f64(x):
    return np.asarray(x).astype(np.float64)


def striped8(idx):
    return np.asarray(idx).reshape(8, -1, 16).transpose(0, 2, 1).reshape(128, -1).astype(np.uint16)


def unstriped8(offs):
    return offs.reshape(8, 16, -1).transpose(0, 2, 1).reshape(8, -1).astype(np.int64)


def pick8(x, idx, run):
    r = np.arange(len(x))
    return x[r[:, None], idx[r % (8 * run) // run]]


E2M1 = np.array([0.0, 0.5, 1.0, 1.5, 2.0, 3.0, 4.0, 6.0, -0.0, -0.5, -1.0, -1.5, -2.0, -3.0, -4.0, -6.0])


def pack_weight(w, fmt):
    k, n = w.shape
    w = f64(np.asarray(w, np.float32).astype(ml_dtypes.bfloat16)).reshape(k // 32, 32, n)
    amax = np.abs(w).max(1)
    if fmt == "e4m3":
        byte = np.frexp(amax)[1] - 1 + 127 - 7
    else:
        mant, ex = np.frexp(amax / 6.0)
        byte = np.where(mant > 0.5, ex, ex - 1) + 127
    byte = np.clip(np.where(amax > 0, byte, 1), 1, 254)
    scaled = (w * np.exp2(127.0 - byte)[:, None, :]).reshape(k, n).astype(np.float32)
    by_word = np.ascontiguousarray(scaled.reshape(k // 512, 128, 4, n).transpose(0, 1, 3, 2))
    if fmt == "e4m3":
        words = by_word.astype(ml_dtypes.float8_e4m3fn).view(np.uint8)
    else:
        c = by_word.astype(ml_dtypes.float4_e2m1fn).view(np.uint8) & 0xF
        words = (c[..., 0::2] | (c[..., 1::2] << 4)).reshape(k // 512, 128, 2 * n)
    return np.ascontiguousarray(words), np.ascontiguousarray(byte.astype(np.uint8).reshape(k // 512, 16, n))


def unpack_weight(words, scales, fmt):
    g, _, n = scales.shape
    words = np.ascontiguousarray(words).reshape(g, 128, n, -1)
    if fmt == "e4m3":
        vals = words.view(ml_dtypes.float8_e4m3fn).astype(np.float64)
    else:
        nib = np.empty((g, 128, n, 4), np.uint8)
        nib[..., 0::2] = words & 0xF
        nib[..., 1::2] = words >> 4
        vals = E2M1[nib]
    vals = vals * np.repeat(np.exp2(scales.astype(np.float64) - 127.0), 8, axis=1)[..., None]
    return vals.transpose(0, 1, 3, 2).reshape(g * 512, n)


def softplus(v):
    return np.log(1.0 + np.exp(v))


D, T, I, Q = 512, 1024, 512, 128


def setup_inputs():
    n = np.random.standard_normal
    idx = np.stack([np.random.permutation(T)[:I] for _ in range(8)])
    idx2 = np.stack([np.random.permutation(T)[:I] for _ in range(8)])
    idx3 = np.stack([np.random.permutation(T)[:I] for _ in range(8)])
    idx4 = np.stack([np.random.permutation(T)[:I] for _ in range(8)])
    fd = mx_kscale(D)
    keysp = pack_weight(n((D, T)) / fd[:, None], "e2m1")
    return {
        "query": (n((D, Q)) * 0.9 / np.sqrt(D) * fd[:, None]).astype(np.float32),
        "query2": (n((D, Q)) * 0.9 / np.sqrt(D) * fd[:, None]).astype(np.float32),
        "keys_words": keysp[0],
        "keys_scales": keysp[1],
        "lam": (np.random.uniform(0.6, 1.2, (Q, 1))).astype(np.float32),
        "old": (np.random.uniform(0.3, 1.7, (Q, T))).astype(np.float32),
        "base": (0.5 * n((Q, T))).astype(np.float32),
        "offs": striped8(idx),
        "offs2": striped8(idx2),
        "offs3": striped8(idx3),
        "offs4": striped8(idx4),
    }


def reference(query, query2, keys_words, keys_scales, lam, old, base, offs, offs2, offs3, offs4):
    idx = unstriped8(offs)
    idx2 = unstriped8(offs2)
    idx3 = unstriped8(offs3)
    idx4 = unstriped8(offs4)
    keysu = unpack_weight(keys_words, keys_scales, "e2m1")
    queryq = mxq(f64(query), 0, "e4m3")
    a = queryq.T @ keysu
    query2q = mxq(f64(query2), 0, "e4m3")
    b = query2q.T @ keysu
    w = pick8(a, idx, 16) / (softplus(pick8(b, idx2, 16)) + 0.5) * f64(lam)
    ws = w * pick8(f64(old), idx3, 16)
    f1 = np.zeros((Q, T))
    f1[np.arange(Q)[:, None], idx4[np.arange(Q) % 128 // 16]] = ws
    y = f64(base) + f1
    return y

@@ -1,0 +1,152 @@
+from contextlib import ExitStack
+
+import concourse.mybir as mybir
+
+D, T, I, Q = 512, 1024, 512, 128
+FLOPS = 2 * 2 * D * T * Q
+
+F32 = mybir.dt.float32
+BF16 = mybir.dt.bfloat16
+I32 = mybir.dt.int32
+U32 = mybir.dt.uint32
+U16 = mybir.dt.uint16
+U8 = mybir.dt.uint8
+FP8X4 = mybir.dt.float8_e4m3fn_x4
+FP4X4 = mybir.dt.float4_e2m1fn_x4
+ALU = mybir.AluOpType
+ACT = mybir.ActivationFunctionType
+
+P = 128
+PACK = 4
+BANK = 512
+LANES = 16
+EXP_CAP = 2.0 ** 60
+Q_SPLIT = 80
+CHUNKS = ((0, 128), (128, 512))
+
+
+def tile_attend_worthfor_lean_timesold_heads_kernel(
+    tc, query, query2, keys_words, keys_scales, lam, old, base, offs, offs2, offs3, offs4, out
+):
+    nc = tc.nc
+    with ExitStack() as ctx:
+        lists = ctx.enter_context(tc.tile_pool(name="lists", bufs=1))
+        sb = ctx.enter_context(tc.tile_pool(name="sb", bufs=1))
+        psum = ctx.enter_context(tc.psum_pool(name="psum", bufs=1))
+
+        key_scales = sb.tile([P, T], U8, align_bytes=64)
+        nc.vector.memset(key_scales[:].bitcast(I32), 0)
+        f1 = sb.tile([P, T], F32)
+        nc.gpsimd.memset(f1[:], 0.0)
+
+        q2_raw = sb.tile([P, PACK, Q], F32)
+        nc.sync.dma_start(out=q2_raw[:], in_=query2.rearrange("(p j) w -> p j w", j=PACK))
+        key_words = sb.tile([P, 2 * T], U8, align_bytes=64)
+        nc.sync.dma_start(out=key_words[:].bitcast(I32), in_=keys_words[0].bitcast(I32))
+        for quad in range(4):
+            nc.sync.dma_start(
+                out=key_scales[32 * quad : 32 * quad + 4, :].bitcast(I32),
+                in_=keys_scales[0, 4 * quad : 4 * quad + 4, :].bitcast(I32),
+            )
+        old_sb = sb.tile([P, T], F32)
+        nc.sync.dma_start(out=old_sb[:], in_=old)
+        list_old = lists.tile([P, I // LANES], U16, name="list_old")
+        nc.sync.dma_start(list_old[:], offs3)
+        q_raw = sb.tile([P, PACK, Q], F32)
+        nc.sync.dma_start(out=q_raw[:], in_=query.rearrange("(p j) w -> p j w", j=PACK))
+        list_b = lists.tile([P, I // LANES], U16, name="list_b")
+        nc.sync.dma_start(list_b[:], offs2)
+        lam_sb = sb.tile([P, 1], F32)
+        nc.sync.dma_start(out=lam_sb[:], in_=lam)
+        list_a = lists.tile([P, I // LANES], U16, name="list_a")
+        nc.sync.dma_start(list_a[:], offs)
+        list_out = lists.tile([P, I // LANES], U16, name="list_out")
+        nc.sync.dma_start(list_out[:], offs4)
+        base_sb = sb.tile([P, T], F32)
+        nc.sync.dma_start(out=base_sb[:], in_=base)
+
+        def entries(lst, lo, hi):
+            return lst[:, lo // LANES : hi // LANES]
+
+        def quantise(grouped, name):
+            codes = sb.tile([P, Q], U32, align_bytes=64, name=name + "_codes")
+            scales = sb.tile([P, Q], U8, align_bytes=64, name=name + "_scales")
+            nc.vector.quantize_mx(
+                out=codes[:].bitcast(FP8X4), scales=scales[:], in_=grouped[:].rearrange("p w j -> p (w j)")
+            )
+            return codes, scales
+
+        def score(codes, scales, name):
+            banks = []
+            for n0 in range(0, T, BANK):
+                bank = psum.tile([P, BANK], F32, name="%s_bank%d" % (name, n0))
+                nc.tensor.matmul_mx(
+                    out=bank[:],
+                    lhsT=codes[:].bitcast(FP8X4),
+                    lhsT_scale=scales[:],
+                    rhs=key_words[:, 2 * n0 : 2 * (n0 + BANK)].bitcast(FP4X4),
+                    rhs_scale=key_scales[:, n0 : n0 + BANK],
+                    start=True,
+                    stop=True,
+                )
+                banks.append(bank)
+            return banks
+
+        q2_grouped = sb.tile([P, Q, PACK], BF16, align_bytes=64)
+        q2_by_column = q2_raw[:].rearrange("p j w -> p w j")
+        nc.vector.tensor_copy(out=q2_grouped[:, :Q_SPLIT, :], in_=q2_by_column[:, :Q_SPLIT, :])
+        nc.scalar.activation(q2_grouped[:, Q_SPLIT:, :], q2_by_column[:, Q_SPLIT:, :], ACT.Copy)
+        q2_codes, q2_scales = quantise(q2_grouped, "q2")
+        b_banks = score(q2_codes, q2_scales, "b")
+
+        old_picked = sb.tile([P, I], F32)
+        nc.scalar.activation(old_picked[:], old_sb[:].indirect(list_old[:]), ACT.Copy)
+
+        b_sb = sb.tile([P, T], F32)
+        nc.vector.tensor_copy(out=b_sb[:, :BANK], in_=b_banks[0][:])
+        q_grouped = sb.tile([P, Q, PACK], BF16, align_bytes=64)
+        nc.vector.tensor_copy(out=q_grouped[:], in_=q_raw[:].rearrange("p j w -> p w j"))
+        nc.vector.tensor_copy(out=b_sb[:, BANK:], in_=b_banks[1][:])
+        q_codes, q_scales = quantise(q_grouped, "q")
+        a_banks = score(q_codes, q_scales, "a")
+
+        half = I // 2
+        exp_b = sb.tile([P, I], F32, tag="exp_then_old")
+        b_picked = sb.tile([P, I], F32)
+        nc.vector.tensor_copy(out=b_picked[:, :half], in_=b_sb[:].indirect(entries(list_b, 0, half)))
+        nc.scalar.activation(exp_b[:, half:], b_sb[:].indirect(entries(list_b, half, I)), ACT.Exp)
+        nc.scalar.activation(exp_b[:, :half], b_picked[:, :half], ACT.Exp)
+        nc.vector.tensor_copy(out=b_picked[:, half:], in_=b_sb[:].indirect(entries(list_b, half, I)))
+
+        exp_capped = sb.tile([P, I], F32)
+        nc.vector.tensor_scalar(exp_capped[:], exp_b[:], EXP_CAP, 1.0, ALU.min, ALU.add)
+
+        a_sb = sb.tile([P, T], F32)
+        for n, bank in enumerate(a_banks):
+            nc.vector.tensor_copy(out=a_sb[:, n * BANK : (n + 1) * BANK], in_=bank[:])
+
+        log_b = sb.tile([P, I], F32)
+        nc.scalar.activation(log_b[:], exp_capped[:], ACT.Ln)
+        old_lam = sb.tile([P, I], F32, tag="exp_then_old")
+        nc.gpsimd.tensor_scalar(old_lam[:], old_picked[:], lam_sb[:, 0:1], 0.0, ALU.mult, ALU.add)
+
+        numer = sb.tile([P, I], F32)
+        nc.vector.tensor_tensor(numer[:], a_sb[:].indirect(list_a[:]), old_lam[:], ALU.mult)
+
+        softplus = sb.tile([P, I], F32)
+        nc.vector.tensor_tensor(softplus[:], log_b[:], b_picked[:], ALU.max)
+
+        root = sb.tile([P, I], F32)
+        recip = sb.tile([P, I], F32)
+        for lo, hi in CHUNKS:
+            nc.scalar.activation(root[:, lo:hi], softplus[:, lo:hi], ACT.Abs_reciprocal_sqrt, bias=0.5)
+            nc.scalar.activation(recip[:, lo:hi], root[:, lo:hi], ACT.Square)
+            nc.vector.tensor_tensor(
+                f1[:].indirect(entries(list_out, lo, hi)), numer[:, lo:hi], recip[:, lo:hi], ALU.mult
+            )
+
+        result = sb.tile([P, T], F32)
+        for n0 in range(0, T, BANK):
+            cols = slice(n0, n0 + BANK)
+            nc.vector.tensor_tensor(result[:, cols], f1[:, cols], base_sb[:, cols], ALU.add)
+            nc.sync.dma_start(out=out[:, cols], in_=result[:, cols])

@@ -20,9 +20,13 @@ P = 128
 PACK = 4
 BANK = 512
 LANES = 16
-EXP_CAP = 2.0 ** 60
+LOG_CAP = 41.0
 Q_SPLIT = 80
+B_PIECES = ((0, 256), (256, 512), (512, 768), (768, 1024))
+A_PIECES = ((0, 512), (512, 1024))
+ROOT_PIECES = ((0, 128), (128, 384), (384, 512))
 CHUNKS = ((0, 128), (128, 512))
+OUT_PIECES = ((0, 384), (384, 768), (768, 1024))
 
 
 def tile_attend_worthfor_lean_timesold_heads_kernel(
@@ -39,6 +43,11 @@ def tile_attend_worthfor_lean_timesold_heads_kernel(
         f1 = sb.tile([P, T], F32)
         nc.gpsimd.memset(f1[:], 0.0)
 
+        def load_list(source, name):
+            tile = lists.tile([P, I // LANES], U16, name=name)
+            nc.sync.dma_start(tile[:], source)
+            return tile
+
         q2_raw = sb.tile([P, PACK, Q], F32)
         nc.sync.dma_start(out=q2_raw[:], in_=query2.rearrange("(p j) w -> p j w", j=PACK))
         key_words = sb.tile([P, 2 * T], U8, align_bytes=64)
@@ -48,20 +57,16 @@ def tile_attend_worthfor_lean_timesold_heads_kernel(
                 out=key_scales[32 * quad : 32 * quad + 4, :].bitcast(I32),
                 in_=keys_scales[0, 4 * quad : 4 * quad + 4, :].bitcast(I32),
             )
-        old_sb = sb.tile([P, T], F32)
-        nc.sync.dma_start(out=old_sb[:], in_=old)
-        list_old = lists.tile([P, I // LANES], U16, name="list_old")
-        nc.sync.dma_start(list_old[:], offs3)
         q_raw = sb.tile([P, PACK, Q], F32)
         nc.sync.dma_start(out=q_raw[:], in_=query.rearrange("(p j) w -> p j w", j=PACK))
-        list_b = lists.tile([P, I // LANES], U16, name="list_b")
-        nc.sync.dma_start(list_b[:], offs2)
+        list_b = load_list(offs2, "list_b")
+        old_sb = sb.tile([P, T], F32, tag="old_then_a")
+        nc.sync.dma_start(out=old_sb[:], in_=old)
+        list_old = load_list(offs3, "list_old")
         lam_sb = sb.tile([P, 1], F32)
         nc.sync.dma_start(out=lam_sb[:], in_=lam)
-        list_a = lists.tile([P, I // LANES], U16, name="list_a")
-        nc.sync.dma_start(list_a[:], offs)
-        list_out = lists.tile([P, I // LANES], U16, name="list_out")
-        nc.sync.dma_start(list_out[:], offs4)
+        list_a = load_list(offs, "list_a")
+        list_out = load_list(offs4, "list_out")
         base_sb = sb.tile([P, T], F32)
         nc.sync.dma_start(out=base_sb[:], in_=base)
 
@@ -69,23 +74,23 @@ def tile_attend_worthfor_lean_timesold_heads_kernel(
             return lst[:, lo // LANES : hi // LANES]
 
         def quantise(grouped, name):
-            codes = sb.tile([P, Q], U32, align_bytes=64, name=name + "_codes")
+            codes = sb.tile([P, Q], U32, align_bytes=64, name=name + "_codes", tag=name + "_codes")
             scales = sb.tile([P, Q], U8, align_bytes=64, name=name + "_scales")
             nc.vector.quantize_mx(
                 out=codes[:].bitcast(FP8X4), scales=scales[:], in_=grouped[:].rearrange("p w j -> p (w j)")
             )
             return codes, scales
 
-        def score(codes, scales, name):
+        def score(codes, scales, pieces, name):
             banks = []
-            for n0 in range(0, T, BANK):
-                bank = psum.tile([P, BANK], F32, name="%s_bank%d" % (name, n0))
+            for lo, hi in pieces:
+                bank = psum.tile([P, hi - lo], F32, name="%s_bank%d" % (name, lo))
                 nc.tensor.matmul_mx(
                     out=bank[:],
                     lhsT=codes[:].bitcast(FP8X4),
                     lhsT_scale=scales[:],
-                    rhs=key_words[:, 2 * n0 : 2 * (n0 + BANK)].bitcast(FP4X4),
-                    rhs_scale=key_scales[:, n0 : n0 + BANK],
+                    rhs=key_words[:, 2 * lo : 2 * hi].bitcast(FP4X4),
+                    rhs_scale=key_scales[:, lo:hi],
                     start=True,
                     stop=True,
                 )
@@ -97,56 +102,57 @@ def tile_attend_worthfor_lean_timesold_heads_kernel(
         nc.vector.tensor_copy(out=q2_grouped[:, :Q_SPLIT, :], in_=q2_by_column[:, :Q_SPLIT, :])
         nc.scalar.activation(q2_grouped[:, Q_SPLIT:, :], q2_by_column[:, Q_SPLIT:, :], ACT.Copy)
         q2_codes, q2_scales = quantise(q2_grouped, "q2")
-        b_banks = score(q2_codes, q2_scales, "b")
+        b_banks = score(q2_codes, q2_scales, B_PIECES, "b")
 
-        old_picked = sb.tile([P, I], F32)
-        nc.scalar.activation(old_picked[:], old_sb[:].indirect(list_old[:]), ACT.Copy)
-
-        b_sb = sb.tile([P, T], F32)
-        nc.vector.tensor_copy(out=b_sb[:, :BANK], in_=b_banks[0][:])
         q_grouped = sb.tile([P, Q, PACK], BF16, align_bytes=64)
         nc.vector.tensor_copy(out=q_grouped[:], in_=q_raw[:].rearrange("p j w -> p w j"))
-        nc.vector.tensor_copy(out=b_sb[:, BANK:], in_=b_banks[1][:])
         q_codes, q_scales = quantise(q_grouped, "q")
-        a_banks = score(q_codes, q_scales, "a")
+        a_banks = score(q_codes, q_scales, A_PIECES, "a")
+
+        b_sb = sb.tile([P, T], F32)
+        for n, (lo, hi) in enumerate(B_PIECES):
+            if n == len(B_PIECES) - 1:
+                nc.vector.tensor_copy(out=b_sb[:, lo:hi], in_=b_banks[n][:])
+            else:
+                nc.scalar.copy(b_sb[:, lo:hi], b_banks[n][:])
 
         half = I // 2
-        exp_b = sb.tile([P, I], F32, tag="exp_then_old")
+        exp_b = sb.tile([P, I], F32, tag="exp_then_numer")
         b_picked = sb.tile([P, I], F32)
         nc.vector.tensor_copy(out=b_picked[:, :half], in_=b_sb[:].indirect(entries(list_b, 0, half)))
         nc.scalar.activation(exp_b[:, half:], b_sb[:].indirect(entries(list_b, half, I)), ACT.Exp)
         nc.scalar.activation(exp_b[:, :half], b_picked[:, :half], ACT.Exp)
         nc.vector.tensor_copy(out=b_picked[:, half:], in_=b_sb[:].indirect(entries(list_b, half, I)))
-
-        exp_capped = sb.tile([P, I], F32)
-        nc.vector.tensor_scalar(exp_capped[:], exp_b[:], EXP_CAP, 1.0, ALU.min, ALU.add)
-
-        a_sb = sb.tile([P, T], F32)
-        for n, bank in enumerate(a_banks):
-            nc.vector.tensor_copy(out=a_sb[:, n * BANK : (n + 1) * BANK], in_=bank[:])
-
         log_b = sb.tile([P, I], F32)
-        nc.scalar.activation(log_b[:], exp_capped[:], ACT.Ln)
-        old_lam = sb.tile([P, I], F32, tag="exp_then_old")
+        nc.scalar.activation(log_b[:], exp_b[:], ACT.Ln, bias=1.0)
+
+        old_picked = sb.tile([P, I], F32, align_bytes=64, tag="q_codes")
+        nc.vector.tensor_copy(out=old_picked[:], in_=old_sb[:].indirect(list_old[:]))
+        old_lam = sb.tile([P, I], F32)
         nc.gpsimd.tensor_scalar(old_lam[:], old_picked[:], lam_sb[:, 0:1], 0.0, ALU.mult, ALU.add)
+        a_sb = sb.tile([P, T], F32, tag="old_then_a")
+        for n, (lo, hi) in enumerate(A_PIECES):
+            nc.vector.tensor_copy(out=a_sb[:, lo:hi], in_=a_banks[n][:])
 
-        numer = sb.tile([P, I], F32)
+        softplus = sb.tile([P, I], F32, align_bytes=64, tag="q_codes")
+        nc.vector.scalar_tensor_tensor(softplus[:], log_b[:], LOG_CAP, b_picked[:], ALU.min, ALU.max)
+
+        numer = sb.tile([P, I], F32, tag="exp_then_numer")
         nc.vector.tensor_tensor(numer[:], a_sb[:].indirect(list_a[:]), old_lam[:], ALU.mult)
-
-        softplus = sb.tile([P, I], F32)
-        nc.vector.tensor_tensor(softplus[:], log_b[:], b_picked[:], ALU.max)
 
         root = sb.tile([P, I], F32)
         recip = sb.tile([P, I], F32)
         for lo, hi in CHUNKS:
-            nc.scalar.activation(root[:, lo:hi], softplus[:, lo:hi], ACT.Abs_reciprocal_sqrt, bias=0.5)
+            for r0, r1 in ROOT_PIECES:
+                if lo <= r0 < hi:
+                    nc.scalar.activation(root[:, r0:r1], softplus[:, r0:r1], ACT.Abs_reciprocal_sqrt, bias=0.5)
             nc.scalar.activation(recip[:, lo:hi], root[:, lo:hi], ACT.Square)
             nc.vector.tensor_tensor(
                 f1[:].indirect(entries(list_out, lo, hi)), numer[:, lo:hi], recip[:, lo:hi], ALU.mult
             )
 
         result = sb.tile([P, T], F32)
-        for n0 in range(0, T, BANK):
-            cols = slice(n0, n0 + BANK)
+        for lo, hi in OUT_PIECES:
+            cols = slice(lo, hi)
             nc.vector.tensor_tensor(result[:, cols], f1[:, cols], base_sb[:, cols], ALU.add)
             nc.sync.dma_start(out=out[:, cols], in_=result[:, cols])

@@ -21,8 +21,9 @@ PACK = 4
 BANK = 512
 LANES = 16
 LOG_CAP = 41.0
+RUN = 4
 Q_SPLIT = 80
-B_PIECES = ((0, 256), (256, 512), (512, 768), (768, 1024))
+B_PIECES = ((0, 256), (256, 512), (512, 768), (768, 896), (896, 1024))
 A_PIECES = ((0, 512), (512, 1024))
 ROOT_PIECES = ((0, 128), (128, 384), (384, 512))
 CHUNKS = ((0, 128), (128, 512))
@@ -41,7 +42,7 @@ def tile_attend_worthfor_lean_timesold_heads_kernel(
         key_scales = sb.tile([P, T], U8, align_bytes=64)
         nc.vector.memset(key_scales[:].bitcast(I32), 0)
         f1 = sb.tile([P, T], F32)
-        nc.gpsimd.memset(f1[:], 0.0)
+        nc.vector.memset(f1[:], 0.0)
 
         def load_list(source, name):
             tile = lists.tile([P, I // LANES], U16, name=name)
@@ -73,6 +74,12 @@ def tile_attend_worthfor_lean_timesold_heads_kernel(
         def entries(lst, lo, hi):
             return lst[:, lo // LANES : hi // LANES]
 
+        def interleaved(grouped, raw, lo, hi):
+            return (
+                grouped[:, lo:hi, :].rearrange("p (c i) j -> p c j i", i=RUN),
+                raw[:, :, lo:hi].rearrange("p j (c i) -> p c j i", i=RUN),
+            )
+
         def quantise(grouped, name):
             codes = sb.tile([P, Q], U32, align_bytes=64, name=name + "_codes", tag=name + "_codes")
             scales = sb.tile([P, Q], U8, align_bytes=64, name=name + "_scales")
@@ -98,14 +105,13 @@ def tile_attend_worthfor_lean_timesold_heads_kernel(
             return banks
 
         q2_grouped = sb.tile([P, Q, PACK], BF16, align_bytes=64)
-        q2_by_column = q2_raw[:].rearrange("p j w -> p w j")
-        nc.vector.tensor_copy(out=q2_grouped[:, :Q_SPLIT, :], in_=q2_by_column[:, :Q_SPLIT, :])
-        nc.scalar.activation(q2_grouped[:, Q_SPLIT:, :], q2_by_column[:, Q_SPLIT:, :], ACT.Copy)
+        nc.vector.tensor_copy(*interleaved(q2_grouped, q2_raw, 0, Q_SPLIT))
+        nc.scalar.activation(*interleaved(q2_grouped, q2_raw, Q_SPLIT, Q), ACT.Copy)
         q2_codes, q2_scales = quantise(q2_grouped, "q2")
         b_banks = score(q2_codes, q2_scales, B_PIECES, "b")
 
         q_grouped = sb.tile([P, Q, PACK], BF16, align_bytes=64)
-        nc.vector.tensor_copy(out=q_grouped[:], in_=q_raw[:].rearrange("p j w -> p w j"))
+        nc.vector.tensor_copy(*interleaved(q_grouped, q_raw, 0, Q))
         q_codes, q_scales = quantise(q_grouped, "q")
         a_banks = score(q_codes, q_scales, A_PIECES, "a")
 

@@ -25,8 +25,8 @@ RUN = 4
 Q_SPLIT = 80
 B_PIECES = ((0, 256), (256, 512), (512, 768), (768, 896), (896, 1024))
 A_PIECES = ((0, 512), (512, 1024))
-ROOT_PIECES = ((0, 128), (128, 384), (384, 512))
-CHUNKS = ((0, 128), (128, 512))
+FIRST = 128
+REST_PIECES = ((128, 320), (320, 512))
 OUT_PIECES = ((0, 384), (384, 768), (768, 1024))
 
 
@@ -141,18 +141,24 @@ def tile_attend_worthfor_lean_timesold_heads_kernel(
             nc.vector.tensor_copy(out=a_sb[:, lo:hi], in_=a_banks[n][:])
 
         softplus = sb.tile([P, I], F32, align_bytes=64, tag="q_codes")
-        nc.vector.scalar_tensor_tensor(softplus[:], log_b[:], LOG_CAP, b_picked[:], ALU.min, ALU.max)
+        for lo, hi in ((0, FIRST), (FIRST, I)):
+            nc.vector.scalar_tensor_tensor(
+                softplus[:, lo:hi], log_b[:, lo:hi], LOG_CAP, b_picked[:, lo:hi], ALU.min, ALU.max
+            )
+        squared = sb.tile([P, FIRST], F32)
+        nc.vector.scalar_tensor_tensor(squared[:], softplus[:, :FIRST], 1.0, softplus[:, :FIRST], ALU.add, ALU.mult)
 
         numer = sb.tile([P, I], F32, tag="exp_then_numer")
         nc.vector.tensor_tensor(numer[:], a_sb[:].indirect(list_a[:]), old_lam[:], ALU.mult)
 
-        root = sb.tile([P, I], F32)
         recip = sb.tile([P, I], F32)
-        for lo, hi in CHUNKS:
-            for r0, r1 in ROOT_PIECES:
-                if lo <= r0 < hi:
-                    nc.scalar.activation(root[:, r0:r1], softplus[:, r0:r1], ACT.Abs_reciprocal_sqrt, bias=0.5)
+        nc.scalar.activation(recip[:, :FIRST], squared[:], ACT.Abs_reciprocal_sqrt, bias=0.25)
+        root = sb.tile([P, I], F32)
+        for lo, hi in REST_PIECES:
+            nc.scalar.activation(root[:, lo:hi], softplus[:, lo:hi], ACT.Abs_reciprocal_sqrt, bias=0.5)
+        for lo, hi in REST_PIECES:
             nc.scalar.activation(recip[:, lo:hi], root[:, lo:hi], ACT.Square)
+        for lo, hi in ((0, FIRST), (FIRST, I)):
             nc.vector.tensor_tensor(
                 f1[:].indirect(entries(list_out, lo, hi)), numer[:, lo:hi], recip[:, lo:hi], ALU.mult
             )

from contextlib import ExitStack

import concourse.mybir as mybir

D, T, I, Q = 512, 1024, 512, 128
FLOPS = 2 * 2 * D * T * Q

F32 = mybir.dt.float32
BF16 = mybir.dt.bfloat16
I32 = mybir.dt.int32
U32 = mybir.dt.uint32
U16 = mybir.dt.uint16
U8 = mybir.dt.uint8
FP8X4 = mybir.dt.float8_e4m3fn_x4
FP4X4 = mybir.dt.float4_e2m1fn_x4
ALU = mybir.AluOpType
ACT = mybir.ActivationFunctionType

P = 128
PACK = 4
BANK = 512
LANES = 16
LOG_CAP = 41.0
RUN = 4
Q_SPLIT = 80
B_PIECES = ((0, 256), (256, 512), (512, 768), (768, 896), (896, 1024))
A_PIECES = ((0, 512), (512, 1024))
FIRST = 128
REST_PIECES = ((128, 320), (320, 512))
OUT_PIECES = ((0, 384), (384, 768), (768, 1024))


def tile_attend_worthfor_lean_timesold_heads_kernel(
    tc, query, query2, keys_words, keys_scales, lam, old, base, offs, offs2, offs3, offs4, out
):
    nc = tc.nc
    with ExitStack() as ctx:
        lists = ctx.enter_context(tc.tile_pool(name="lists", bufs=1))
        sb = ctx.enter_context(tc.tile_pool(name="sb", bufs=1))
        psum = ctx.enter_context(tc.psum_pool(name="psum", bufs=1))

        key_scales = sb.tile([P, T], U8, align_bytes=64)
        nc.vector.memset(key_scales[:].bitcast(I32), 0)
        f1 = sb.tile([P, T], F32)
        nc.vector.memset(f1[:], 0.0)

        def load_list(source, name):
            tile = lists.tile([P, I // LANES], U16, name=name)
            nc.sync.dma_start(tile[:], source)
            return tile

        q2_raw = sb.tile([P, PACK, Q], F32)
        nc.sync.dma_start(out=q2_raw[:], in_=query2.rearrange("(p j) w -> p j w", j=PACK))
        key_words = sb.tile([P, 2 * T], U8, align_bytes=64)
        nc.sync.dma_start(out=key_words[:].bitcast(I32), in_=keys_words[0].bitcast(I32))
        for quad in range(4):
            nc.sync.dma_start(
                out=key_scales[32 * quad : 32 * quad + 4, :].bitcast(I32),
                in_=keys_scales[0, 4 * quad : 4 * quad + 4, :].bitcast(I32),
            )
        q_raw = sb.tile([P, PACK, Q], F32)
        nc.sync.dma_start(out=q_raw[:], in_=query.rearrange("(p j) w -> p j w", j=PACK))
        list_b = load_list(offs2, "list_b")
        old_sb = sb.tile([P, T], F32, tag="old_then_a")
        nc.sync.dma_start(out=old_sb[:], in_=old)
        list_old = load_list(offs3, "list_old")
        lam_sb = sb.tile([P, 1], F32)
        nc.sync.dma_start(out=lam_sb[:], in_=lam)
        list_a = load_list(offs, "list_a")
        list_out = load_list(offs4, "list_out")
        base_sb = sb.tile([P, T], F32)
        nc.sync.dma_start(out=base_sb[:], in_=base)

        def entries(lst, lo, hi):
            return lst[:, lo // LANES : hi // LANES]

        def interleaved(grouped, raw, lo, hi):
            return (
                grouped[:, lo:hi, :].rearrange("p (c i) j -> p c j i", i=RUN),
                raw[:, :, lo:hi].rearrange("p j (c i) -> p c j i", i=RUN),
            )

        def quantise(grouped, name):
            codes = sb.tile([P, Q], U32, align_bytes=64, name=name + "_codes", tag=name + "_codes")
            scales = sb.tile([P, Q], U8, align_bytes=64, name=name + "_scales")
            nc.vector.quantize_mx(
                out=codes[:].bitcast(FP8X4), scales=scales[:], in_=grouped[:].rearrange("p w j -> p (w j)")
            )
            return codes, scales

        def score(codes, scales, pieces, name):
            banks = []
            for lo, hi in pieces:
                bank = psum.tile([P, hi - lo], F32, name="%s_bank%d" % (name, lo))
                nc.tensor.matmul_mx(
                    out=bank[:],
                    lhsT=codes[:].bitcast(FP8X4),
                    lhsT_scale=scales[:],
                    rhs=key_words[:, 2 * lo : 2 * hi].bitcast(FP4X4),
                    rhs_scale=key_scales[:, lo:hi],
                    start=True,
                    stop=True,
                )
                banks.append(bank)
            return banks

        q2_grouped = sb.tile([P, Q, PACK], BF16, align_bytes=64)
        nc.vector.tensor_copy(*interleaved(q2_grouped, q2_raw, 0, Q_SPLIT))
        nc.scalar.activation(*interleaved(q2_grouped, q2_raw, Q_SPLIT, Q), ACT.Copy)
        q2_codes, q2_scales = quantise(q2_grouped, "q2")
        b_banks = score(q2_codes, q2_scales, B_PIECES, "b")

        q_grouped = sb.tile([P, Q, PACK], BF16, align_bytes=64)
        nc.vector.tensor_copy(*interleaved(q_grouped, q_raw, 0, Q))
        q_codes, q_scales = quantise(q_grouped, "q")
        a_banks = score(q_codes, q_scales, A_PIECES, "a")

        b_sb = sb.tile([P, T], F32)
        for n, (lo, hi) in enumerate(B_PIECES):
            if n == len(B_PIECES) - 1:
                nc.vector.tensor_copy(out=b_sb[:, lo:hi], in_=b_banks[n][:])
            else:
                nc.scalar.copy(b_sb[:, lo:hi], b_banks[n][:])

        half = I // 2
        exp_b = sb.tile([P, I], F32, tag="exp_then_numer")
        b_picked = sb.tile([P, I], F32)
        nc.vector.tensor_copy(out=b_picked[:, :half], in_=b_sb[:].indirect(entries(list_b, 0, half)))
        nc.scalar.activation(exp_b[:, half:], b_sb[:].indirect(entries(list_b, half, I)), ACT.Exp)
        nc.scalar.activation(exp_b[:, :half], b_picked[:, :half], ACT.Exp)
        nc.vector.tensor_copy(out=b_picked[:, half:], in_=b_sb[:].indirect(entries(list_b, half, I)))
        log_b = sb.tile([P, I], F32)
        nc.scalar.activation(log_b[:], exp_b[:], ACT.Ln, bias=1.0)

        old_picked = sb.tile([P, I], F32, align_bytes=64, tag="q_codes")
        nc.vector.tensor_copy(out=old_picked[:], in_=old_sb[:].indirect(list_old[:]))
        old_lam = sb.tile([P, I], F32)
        nc.gpsimd.tensor_scalar(old_lam[:], old_picked[:], lam_sb[:, 0:1], 0.0, ALU.mult, ALU.add)
        a_sb = sb.tile([P, T], F32, tag="old_then_a")
        for n, (lo, hi) in enumerate(A_PIECES):
            nc.vector.tensor_copy(out=a_sb[:, lo:hi], in_=a_banks[n][:])

        softplus = sb.tile([P, I], F32, align_bytes=64, tag="q_codes")
        for lo, hi in ((0, FIRST), (FIRST, I)):
            nc.vector.scalar_tensor_tensor(
                softplus[:, lo:hi], log_b[:, lo:hi], LOG_CAP, b_picked[:, lo:hi], ALU.min, ALU.max
            )
        squared = sb.tile([P, FIRST], F32)
        nc.vector.scalar_tensor_tensor(squared[:], softplus[:, :FIRST], 1.0, softplus[:, :FIRST], ALU.add, ALU.mult)

        numer = sb.tile([P, I], F32, tag="exp_then_numer")
        nc.vector.tensor_tensor(numer[:], a_sb[:].indirect(list_a[:]), old_lam[:], ALU.mult)

        recip = sb.tile([P, I], F32)
        nc.scalar.activation(recip[:, :FIRST], squared[:], ACT.Abs_reciprocal_sqrt, bias=0.25)
        root = sb.tile([P, I], F32)
        for lo, hi in REST_PIECES:
            nc.scalar.activation(root[:, lo:hi], softplus[:, lo:hi], ACT.Abs_reciprocal_sqrt, bias=0.5)
        for lo, hi in REST_PIECES:
            nc.scalar.activation(recip[:, lo:hi], root[:, lo:hi], ACT.Square)
        for lo, hi in ((0, FIRST), (FIRST, I)):
            nc.vector.tensor_tensor(
                f1[:].indirect(entries(list_out, lo, hi)), numer[:, lo:hi], recip[:, lo:hi], ALU.mult
            )

        result = sb.tile([P, T], F32)
        for lo, hi in OUT_PIECES:
            cols = slice(lo, hi)
            nc.vector.tensor_tensor(result[:, cols], f1[:, cols], base_sb[:, cols], ALU.add)
            nc.sync.dma_start(out=out[:, cols], in_=result[:, cols])
